import numpy as np
import ml_dtypes


def mxq(x, axis, fmt="e4m3"):
    dtype, down = {"e4m3": (ml_dtypes.float8_e4m3fn, 7), "e5m2": (ml_dtypes.float8_e5m2, 14)}[fmt]
    v = np.moveaxis(np.asarray(x, np.float32).astype(ml_dtypes.bfloat16).astype(np.float64), axis, -1)
    blocks = v.reshape(v.shape[:-1] + (-1, 32))
    amax = np.abs(blocks).max(-1, keepdims=True)
    byte = np.maximum(np.where(amax > 0, np.frexp(amax)[1] - 1 + 127, 0) - down, 1)
    scale = np.exp2(byte - 127.0)
    codes = (blocks / scale).astype(np.float32).astype(dtype).astype(np.float64)
    return np.moveaxis((codes * scale).reshape(v.shape), -1, axis)


WIDE = False


def mx_kscale(k):
    if not WIDE:
        return np.ones(k)
    levels = np.array([10, -10, 5, -5, 0])
    if k % 512:
        return np.exp2(np.random.permutation(np.resize(levels, k // 32))).repeat(32)
    a = np.empty((k // 512, 16))
    for p in range(k // 512):
        a[p, :8] = np.random.permutation(np.resize(levels, 8))
        for g in range(8):
            far = levels[np.abs(levels - a[p, g]) >= 10]
            a[p, g + 8] = far[np.random.randint(len(far))]
    return np.exp2(a.ravel()).repeat(32)


def f64(x):
    return np.asarray(x).astype(np.float64)


def striped(idx):
    return np.tile(idx.reshape(-1, 16).T, (8, 1)).astype(np.uint16)


def unstriped(offs):
    return offs[:16].T.reshape(-1).astype(np.int64)


E2M1 = np.array([0.0, 0.5, 1.0, 1.5, 2.0, 3.0, 4.0, 6.0, -0.0, -0.5, -1.0, -1.5, -2.0, -3.0, -4.0, -6.0])


def pack_weight(w, fmt):
    k, n = w.shape
    w = f64(np.asarray(w, np.float32).astype(ml_dtypes.bfloat16)).reshape(k // 32, 32, n)
    amax = np.abs(w).max(1)
    if fmt == "e4m3":
        byte = np.frexp(amax)[1] - 1 + 127 - 7
    else:
        mant, ex = np.frexp(amax / 6.0)
        byte = np.where(mant > 0.5, ex, ex - 1) + 127
    byte = np.clip(np.where(amax > 0, byte, 1), 1, 254)
    scaled = (w * np.exp2(127.0 - byte)[:, None, :]).reshape(k, n).astype(np.float32)
    by_word = np.ascontiguousarray(scaled.reshape(k // 512, 128, 4, n).transpose(0, 1, 3, 2))
    if fmt == "e4m3":
        words = by_word.astype(ml_dtypes.float8_e4m3fn).view(np.uint8)
    else:
        c = by_word.astype(ml_dtypes.float4_e2m1fn).view(np.uint8) & 0xF
        words = (c[..., 0::2] | (c[..., 1::2] << 4)).reshape(k // 512, 128, 2 * n)
    return np.ascontiguousarray(words), np.ascontiguousarray(byte.astype(np.uint8).reshape(k // 512, 16, n))


def unpack_weight(words, scales, fmt):
    g, _, n = scales.shape
    words = np.ascontiguousarray(words).reshape(g, 128, n, -1)
    if fmt == "e4m3":
        vals = words.view(ml_dtypes.float8_e4m3fn).astype(np.float64)
    else:
        nib = np.empty((g, 128, n, 4), np.uint8)
        nib[..., 0::2] = words & 0xF
        nib[..., 1::2] = words >> 4
        vals = E2M1[nib]
    vals = vals * np.repeat(np.exp2(scales.astype(np.float64) - 127.0), 8, axis=1)[..., None]
    return vals.transpose(0, 1, 3, 2).reshape(g * 512, n)


def gelu(v):
    return 0.5 * v * (1.0 + np.tanh(np.sqrt(2.0 / np.pi) * (v + 0.044715 * v**3)))


def striped8(idx):
    return np.concatenate([v.reshape(-1, 16).T for v in idx]).astype(np.uint16)


def unstriped8(offs):
    return np.stack([offs[16 * g:16 * g + 16].T.reshape(-1) for g in range(8)]).astype(np.int64)


def runs(v, idx8):
    k = np.arange(v.shape[0])
    return v[k[:, None], idx8[k % 512 // 64]]


K, K2, H, N, T, S, T2 = 1024, 512, 1024, 512, 2048, 1024, 2048

def setup_inputs():
    n = np.random.standard_normal
    s = mx_kscale(K)[:, None]
    s2 = mx_kscale(K2)[:, None]
    u = mx_kscale(H)[:, None]
    tab_words, tab_scales = pack_weight(n((K, T)) * s, "e4m3")
    tab2_words, tab2_scales = pack_weight(n((K2, T)) * s2, "e4m3")
    w1_words, w1_scales = pack_weight(n((K, H)) / np.sqrt(K) / s * u.T, "e2m1")
    w2 = (0.36 * n((K2, H)) / np.sqrt(K2) / s2).astype(np.float32)
    b2 = np.random.uniform(-1.1, 1.1, H).astype(np.float32)
    w3 = (n((H, N)) / np.sqrt(H) / u).astype(np.float32)
    page1 = (0.8 * n((N, T2))).astype(np.float32)
    wgo = np.exp(0.3 * n((128, S))).astype(np.float32)
    offs = striped8(np.stack([np.random.permutation(T)[:S] for _ in range(8)]))
    offs2 = striped(np.random.permutation(T)[:S])
    offs3 = striped(np.random.permutation(T2)[:S])
    return {"tab_words": tab_words, "tab_scales": tab_scales, "tab2_words": tab2_words, "tab2_scales": tab2_scales,
            "w1_words": w1_words, "w1_scales": w1_scales, "w2": w2, "b2": b2, "w3": w3,
            "page1": page1, "wgo": wgo, "offs": offs, "offs2": offs2, "offs3": offs3}

def reference(tab_words, tab_scales, tab2_words, tab2_scales, w1_words, w1_scales, w2, b2, w3,
              page1, wgo, offs, offs2, offs3):
    v = runs(unpack_weight(tab_words, tab_scales, "e4m3"), unstriped8(offs))
    v2 = unpack_weight(tab2_words, tab2_scales, "e4m3")[:, unstriped(offs2)]
    w1 = unpack_weight(w1_words, w1_scales, "e2m1")
    cloth = w1.T @ v
    wax = (mxq(f64(w2), 0, "e4m3").T @ v2) + f64(b2)[:, None]
    h = np.maximum(cloth * np.sin(wax), cloth)
    y = mxq(f64(w3), 0, "e4m3").T @ mxq(h, 0, "e4m3")
    out = f64(page1).copy()
    out[:, unstriped(offs3)] = np.tile(f64(wgo), (N // 128, 1)) * y
    return out

@@ -1,0 +1,318 @@
+from contextlib import ExitStack
+
+import concourse.mybir as mybir
+from concourse.masks import make_identity
+
+K, K2, H, N, T, S, T2 = 1024, 512, 1024, 512, 2048, 1024, 2048
+FLOPS = 2 * S * (K * H + K2 * H + H * N)
+
+F32 = mybir.dt.float32
+BF16 = mybir.dt.bfloat16
+I32 = mybir.dt.int32
+U32 = mybir.dt.uint32
+U16 = mybir.dt.uint16
+U8 = mybir.dt.uint8
+FP8X4 = mybir.dt.float8_e4m3fn_x4
+FP4X4 = mybir.dt.float4_e2m1fn_x4
+ALU = mybir.AluOpType
+ACT = mybir.ActivationFunctionType
+
+P = 128
+Q = 256
+HALF = 512
+
+
+def tile_list_wax_crack_scores_kernel(
+    tc, tab_words, tab_scales, tab2_words, tab2_scales, w1_words, w1_scales,
+    w2, b2, w3, page1, wgo, offs, offs2, offs3, out,
+):
+    nc = tc.nc
+    with ExitStack() as ctx:
+        keep = ctx.enter_context(tc.tile_pool(name="keep", bufs=1))
+        ring = ctx.enter_context(tc.tile_pool(name="ring", bufs=3))
+        psum = ctx.enter_context(tc.psum_pool(name="psum", bufs=2))
+
+        def held(shape, dtype, name, tag=""):
+            return keep.tile(shape, dtype, name=name, tag=tag, align_bytes=64)
+
+        list1 = keep.tile([P, S // 16], U16, name="list1")
+        list2 = keep.tile([P, S // 16], U16, name="list2")
+        list3 = keep.tile([P, S // 16], U16, name="list3")
+        tab_sc = held([P, T], U8, "tab_sc", "slot_c")
+        tab2_sc = held([P, T], U8, "tab2_sc", "slot_d")
+        tab2w = held([P, T], I32, "tab2w", "slot_a")
+        tabw = []
+        got_sc = held([P, S], U8, "got_sc")
+        v2_sc = held([P, S], U8, "v2_sc")
+        v_sc = [held([P, S], U8, "v_sc%d" % g) for g in range(2)]
+        v_w = [[held([P, HALF], U32, "v_w%d_%d" % (g, u)) for u in range(2)] for g in range(2)]
+        v2_w = [held([P, HALF], U32, "v2_w%d" % u) for u in range(2)]
+        w1_c = held([P, 2 * H // 2], I32, "w1_c")
+        w1s_raw = held([P, 2 * H // 4], I32, "w1s_raw", "slot_e")
+        w1_s = held([P, 2 * H // 4], I32, "w1_s")
+        w2_raw = [held([P, 4, 512], F32, "w2_raw0", "slot_b")]
+        w3_raw = []
+        page = []
+        w2_c = [held([P, 512], U32, "w2_c%d" % b) for b in range(2)]
+        w2_s = [held([P, 512], U8, "w2_s%d" % b) for b in range(2)]
+        w3_c = [held([P, 512], U32, "w3_c%d" % b) for b in range(2)]
+        w3_s = [held([P, 512], U8, "w3_s%d" % b) for b in range(2)]
+        y_sb = [held([P, 4, HALF], F32, "y_sb%d" % u) for u in range(2)]
+        bias_rows = held([P, P], F32, "bias_rows", "slot_f")
+        ident = held([P, P], F32, "ident")
+        bias = held([P, 8], F32, "bias")
+
+        nc.vector.memset(tab_sc[:].bitcast(I32), 0)
+        nc.gpsimd.memset(tab2_sc[:].bitcast(I32), 0)
+        nc.vector.memset(bias_rows[:], 0.0)
+        make_identity(nc, ident[:])
+        nc.gpsimd.memset(w1s_raw[:], 0)
+        for g in range(2):
+            nc.vector.memset(v_sc[g][:].bitcast(I32), 0)
+
+        def words(dram):
+            return dram.rearrange("p t i -> p (t i)").bitcast(I32)
+
+        def load_w2(b):
+            nc.sync.dma_start(w2_raw[b][:], w2[:, 512 * b : 512 * (b + 1)].rearrange("(p j) c -> p j c", j=4))
+
+        def load_w3(b, tag):
+            w3_raw.append(held([P, 4, 512], F32, "w3_raw%d" % b, tag))
+            rows = w3[512 * b : 512 * (b + 1), :].rearrange("(m t s) n -> s m t n", t=4, s=4)
+            for s in range(4):
+                nc.sync.dma_start(w3_raw[b][s:P:4, :, :], rows[s])
+
+        def load_page(n, tag):
+            page.append(held([P, T2], F32, "page%d" % n, tag))
+            nc.sync.dma_start(page[n][:], page1[P * n : P * (n + 1), :])
+
+        def gather_words(dst, table, lst, u):
+            nc.vector.tensor_copy(dst[:], table[:].bitcast(U32).indirect(lst[:, 32 * u : 32 * (u + 1)]))
+
+        def round_w2(b):
+            grouped = ring.tile([P, 2048], BF16, name="w2_bf", tag="grouped", bufs=2, align_bytes=64)
+            nc.scalar.copy(
+                grouped[:].rearrange("p (t m i j) -> p t m j i", t=4, i=4, j=4),
+                w2_raw[b][:].rearrange("p j (m t i) -> p t m j i", t=4, i=4),
+            )
+            return grouped
+
+        def round_w3(b):
+            grouped = ring.tile([P, 2048], BF16, name="w3_bf", tag="grouped", bufs=2, align_bytes=64)
+            nc.scalar.copy(
+                grouped[:].rearrange("p (c i t) -> p c t i", t=4, i=4),
+                w3_raw[b][:].rearrange("p t (c i) -> p c t i", i=4),
+            )
+            return grouped
+
+        def quantise(codes, scales, grouped):
+            nc.vector.quantize_mx(out=codes.bitcast(FP8X4), scales=scales, in_=grouped)
+
+        sines = {}
+
+        def wax_side(q, b):
+            u, c0 = divmod(q * Q, HALF)
+            sine = held([P, 4, Q], F32, "sine%d_%d" % (q, b))
+            for pair in range(2):
+                wax = psum.tile([P, 2, Q], F32, name="wax", tag="wax")
+                for e in range(2):
+                    t = 2 * pair + e
+                    nc.tensor.matmul_mx(
+                        out=wax[:, e, :],
+                        lhsT=w2_c[b][:, P * t : P * (t + 1)].bitcast(FP8X4),
+                        lhsT_scale=w2_s[b][:, P * t : P * (t + 1)],
+                        rhs=v2_w[u][:, c0 : c0 + Q].bitcast(FP8X4),
+                        rhs_scale=v2_sc[:, q * Q : (q + 1) * Q],
+                        start=True, stop=True,
+                    )
+                for e in range(2):
+                    t = 2 * pair + e
+                    nc.scalar.activation(
+                        sine[:, t, :], wax[:, e, :], ACT.Sin, bias=bias[:, 4 * b + t : 4 * b + t + 1], scale=1.0
+                    )
+            sines[(q, b)] = sine
+
+        nc.sync.dma_start(list1[:], offs)
+        nc.sync.dma_start(list2[:], offs2)
+        for g in range(2):
+            nc.scalar.dma_start(tab_sc[g:P:8, :].bitcast(I32), tab_scales[g].bitcast(I32))
+        nc.sync.dma_start(tab2w[:], words(tab2_words[0]))
+        load_w2(0)
+        nc.sync.dma_start(list3[:], offs3)
+        for b in range(2):
+            nc.scalar.dma_start(
+                bias_rows[4 * b : 4 * b + 4, :].rearrange("t (m s) -> t m s", s=4),
+                b2[512 * b : 512 * (b + 1)].rearrange("(m t s) -> t m s", t=4, s=4),
+            )
+        for d in range(4):
+            nc.scalar.dma_start(
+                tab2_sc[32 * d : 32 * d + 4, :].bitcast(I32), tab2_scales[0, 4 * d : 4 * d + 4, :].bitcast(I32)
+            )
+        for d in range(4):
+            nc.gpsimd.dma_start(
+                w1s_raw[32 * d : 32 * d + 4, :].rearrange("p (g c) -> p g c", g=2),
+                w1_scales[:, 4 * d : 4 * d + 4, :].bitcast(I32).rearrange("g r c -> r g c"),
+            )
+
+        nc.vector.tensor_copy(got_sc[:], tab_sc[:].indirect(list1[:]))
+        tabw.append(held([P, T], I32, "tabw0", "slot_c"))
+        nc.sync.dma_start(tabw[0][:], words(tab_words[0]))
+        turned = psum.tile([P, 2, Q], F32, name="turned", tag="y")
+        nc.tensor.transpose(turned[:, 0, 0:P], bias_rows[:], ident[:])
+        nc.scalar.copy(bias[:], turned[:, 0, 0:8])
+        w1_raw = held([P, 2 * H // 2], I32, "w1_raw", "slot_f")
+        nc.sync.dma_start(
+            w1_raw[:].rearrange("p (g c) -> p g c", g=2), w1_words.bitcast(I32).rearrange("g p c -> p g c")
+        )
+        for g in range(2):
+            for d in range(4):
+                nc.sync.dma_start(
+                    v_sc[g][32 * d : 32 * d + 4, :].bitcast(I32),
+                    got_sc[32 * d + g : 32 * (d + 1) : 8, :].bitcast(I32),
+                )
+        gather_words(v2_w[0], tab2w, list2, 0)
+        gather_words(v2_w[1], tab2w, list2, 1)
+        nc.vector.tensor_copy(v2_sc[:], tab2_sc[:].indirect(list2[:]))
+        tabw.append(held([P, T], I32, "tabw1", "slot_a"))
+        nc.sync.dma_start(tabw[1][:], words(tab_words[1]))
+        w2_bf = round_w2(0)
+        quantise(w2_c[0][:], w2_s[0][:], w2_bf[:])
+        w2_raw.append(held([P, 4, 512], F32, "w2_raw1", "slot_b"))
+        load_w2(1)
+        load_w3(0, "slot_d")
+        gather_words(v_w[0][0], tabw[0], list1, 0)
+        gather_words(v_w[0][1], tabw[0], list1, 1)
+        load_w3(1, "slot_c")
+        w2_bf = round_w2(1)
+        for q in range(4):
+            wax_side(q, 0)
+        gather_words(v_w[1][0], tabw[1], list1, 0)
+        nc.vector.tensor_copy(
+            w1_s[:].rearrange("p (g t m) -> p g t m", t=4, m=32),
+            w1s_raw[:].rearrange("p (g m t) -> p g t m", t=4, m=32),
+        )
+        nc.vector.tensor_copy(
+            w1_c[:].rearrange("p (g t m e) -> p g t m e", t=4, m=32, e=2),
+            w1_raw[:].rearrange("p (g m t e) -> p g t m e", t=4, m=32, e=2),
+        )
+        quantise(w2_c[1][:], w2_s[1][:], w2_bf[:])
+        gather_words(v_w[1][1], tabw[1], list1, 1)
+        gain = held([P, S], F32, "gain", "slot_e")
+        nc.sync.dma_start(gain[:], wgo)
+        load_page(0, "slot_a")
+        load_page(1, "slot_b")
+
+        w1_codes = w1_c[:].bitcast(U8)
+        w1_scale = w1_s[:].bitcast(U8)
+
+        def front(unit):
+            q, b = divmod(unit, 2)
+            u, c0 = divmod(q * Q, HALF)
+            if b == 1:
+                wax_side(q, b)
+            sine = sines[(q, b)]
+            cloth_bf = ring.tile([P, 4 * Q], BF16, name="cloth_bf", align_bytes=64)
+            banks = []
+            for x in range(2):
+                cloth = psum.tile([P, 4, P], F32, name="cloth", tag="cloth", bufs=4)
+                j0 = q * Q + P * x
+                for t in range(4):
+                    for g in range(2):
+                        col = H * g + 512 * b + P * t
+                        nc.tensor.matmul_mx(
+                            out=cloth[:, t, :],
+                            lhsT=w1_codes[:, 2 * col : 2 * (col + P)].bitcast(FP4X4),
+                            lhsT_scale=w1_scale[:, col : col + P],
+                            rhs=v_w[g][u][:, c0 + P * x : c0 + P * (x + 1)].bitcast(FP8X4),
+                            rhs_scale=v_sc[g][:, j0 : j0 + P],
+                            start=(g == 0), stop=(g == 1),
+                        )
+                nc.scalar.copy(
+                    cloth_bf[:, 512 * x : 512 * (x + 1)].rearrange("p (j t) -> p j t", t=4),
+                    cloth[:].rearrange("p t j -> p j t"),
+                )
+                banks.append(cloth)
+            prod = ring.tile([P, 4 * Q], BF16, name="prod", align_bytes=64)
+            return {"sine": sine, "cloth_bf": cloth_bf, "banks": banks, "prod": prod}
+
+        def multiply(st, x):
+            nc.vector.tensor_tensor(
+                st["prod"][:, 512 * x : 512 * (x + 1)].rearrange("p (c i t) -> p c t i", i=2, t=4),
+                st["banks"][x][:].rearrange("p t (c i) -> p c t i", i=2),
+                st["sine"][:, :, P * x : P * (x + 1)].rearrange("p t (c i) -> p c t i", i=2),
+                ALU.mult,
+            )
+
+        def larger(st):
+            h_bf = ring.tile([P, 4 * Q], BF16, name="h_bf", bufs=2, align_bytes=64)
+            nc.vector.tensor_tensor(h_bf[:], st["prod"][:], st["cloth_bf"][:], ALU.max)
+            st["h_bf"] = h_bf
+
+        def quantise_h(st):
+            h_c = ring.tile([P, Q], U32, name="h_c", bufs=4, align_bytes=64)
+            h_s = ring.tile([P, Q], U8, name="h_s", bufs=4, align_bytes=64)
+            quantise(h_c[:], h_s[:], st["h_bf"][:])
+            st["h_c"], st["h_s"] = h_c, h_s
+
+        def second_product(q, pair_of_units):
+            u, c0 = divmod(q * Q, HALF)
+            for pair in range(2):
+                y = psum.tile([P, 2, Q], F32, name="y", tag="y")
+                for e in range(2):
+                    n = 2 * pair + e
+                    for b in range(2):
+                        nc.tensor.matmul_mx(
+                            out=y[:, e, :],
+                            lhsT=w3_c[b][:, P * n : P * (n + 1)].bitcast(FP8X4),
+                            lhsT_scale=w3_s[b][:, P * n : P * (n + 1)],
+                            rhs=pair_of_units[b]["h_c"][:].bitcast(FP8X4),
+                            rhs_scale=pair_of_units[b]["h_s"][:],
+                            start=(b == 0), stop=(b == 1),
+                        )
+                nc.scalar.copy(y_sb[u][:, 2 * pair : 2 * pair + 2, c0 : c0 + Q], y[:])
+
+        def scatter(n, j0, width):
+            u, c0 = divmod(j0, HALF)
+            nc.vector.tensor_tensor(
+                page[n][:].indirect(list3[:, j0 // 16 : (j0 + width) // 16]),
+                y_sb[u][:, n, c0 : c0 + width],
+                gain[:, j0 : j0 + width],
+                ALU.mult,
+            )
+
+        def store(n):
+            nc.sync.dma_start(out[P * n : P * (n + 1), :], page[n][:])
+
+        early = {4: [(0, 0), (1, 0)], 5: [(2, 0), (3, 0)], 6: [(0, 1), (1, 1)], 7: [(2, 1)]}
+        units = [front(0)]
+        for unit in range(8):
+            if unit + 1 < 8:
+                units.append(front(unit + 1))
+            if unit in (0, 1):
+                w3_bf = round_w3(unit)
+                load_page(2 + unit, ("slot_d", "slot_c")[unit])
+            for n, q in early.get(unit, []):
+                scatter(n, q * Q, Q)
+            multiply(units[unit], 0)
+            if unit > 0:
+                larger(units[unit - 1])
+            multiply(units[unit], 1)
+            if unit > 0:
+                quantise_h(units[unit - 1])
+            if unit in (0, 1):
+                quantise(w3_c[unit][:], w3_s[unit][:], w3_bf[:])
+            if unit > 0 and unit % 2 == 0:
+                second_product(unit // 2 - 1, units[unit - 2 : unit])
+        scatter(3, Q, Q)
+        larger(units[7])
+        scatter(0, 2 * Q, Q)
+        quantise_h(units[7])
+        second_product(3, units[6:8])
+        scatter(1, 2 * Q, Q)
+        scatter(0, 3 * Q, Q)
+        store(0)
+        scatter(1, 3 * Q, Q)
+        store(1)
+        for n in (2, 3):
+            scatter(n, 2 * Q, 2 * Q)
+            store(n)

@@ -20,6 +20,7 @@ ACT = mybir.ActivationFunctionType
 P = 128
 Q = 256
 HALF = 512
+UNITS = [(q, b) for b in range(2) for q in range(4)]
 
 
 def tile_list_wax_crack_scores_kernel(
@@ -29,6 +30,7 @@ def tile_list_wax_crack_scores_kernel(
     nc = tc.nc
     with ExitStack() as ctx:
         keep = ctx.enter_context(tc.tile_pool(name="keep", bufs=1))
+        shared = ctx.enter_context(tc.tile_pool(name="shared", bufs=1))
         ring = ctx.enter_context(tc.tile_pool(name="ring", bufs=3))
         psum = ctx.enter_context(tc.psum_pool(name="psum", bufs=2))
 
@@ -38,37 +40,36 @@ def tile_list_wax_crack_scores_kernel(
         list1 = keep.tile([P, S // 16], U16, name="list1")
         list2 = keep.tile([P, S // 16], U16, name="list2")
         list3 = keep.tile([P, S // 16], U16, name="list3")
-        tab_sc = held([P, T], U8, "tab_sc", "slot_c")
-        tab2_sc = held([P, T], U8, "tab2_sc", "slot_d")
-        tab2w = held([P, T], I32, "tab2w", "slot_a")
-        tabw = []
+        tab_sc = shared.tile([P, T], U8, name="tab_sc", offset=7168, align_bytes=64)
+        tab2_sc = shared.tile([P, T], U8, name="tab2_sc", offset=39936, align_bytes=64)
+        tab2w = shared.tile([P, T], I32, name="tab2w", offset=20480, align_bytes=64)
+        tabw = [shared.tile([P, T], I32, name="tabw0", offset=49152, align_bytes=64)]
         got_sc = held([P, S], U8, "got_sc")
         v2_sc = held([P, S], U8, "v2_sc")
         v_sc = [held([P, S], U8, "v_sc%d" % g) for g in range(2)]
         v_w = [[held([P, HALF], U32, "v_w%d_%d" % (g, u)) for u in range(2)] for g in range(2)]
         v2_w = [held([P, HALF], U32, "v2_w%d" % u) for u in range(2)]
         w1_c = held([P, 2 * H // 2], I32, "w1_c")
-        w1s_raw = held([P, 2 * H // 4], I32, "w1s_raw", "slot_e")
+        w1s_raw = shared.tile([P, 2 * H // 4], I32, name="w1s_raw", offset=61440, align_bytes=64)
         w1_s = held([P, 2 * H // 4], I32, "w1_s")
-        w2_raw = [held([P, 4, 512], F32, "w2_raw0", "slot_b")]
+        w2_raw = [held([P, 4, 512], F32, "w2_raw0")]
         w3_raw = []
         page = []
         w2_c = [held([P, 512], U32, "w2_c%d" % b) for b in range(2)]
         w2_s = [held([P, 512], U8, "w2_s%d" % b) for b in range(2)]
         w3_c = [held([P, 512], U32, "w3_c%d" % b) for b in range(2)]
         w3_s = [held([P, 512], U8, "w3_s%d" % b) for b in range(2)]
-        y_sb = [held([P, 4, HALF], F32, "y_sb%d" % u) for u in range(2)]
-        bias_rows = held([P, P], F32, "bias_rows", "slot_f")
+        y_late = held([P, 4, HALF], F32, "y_late")
+        y_early = []
+        bias_rows = held([P, P], F32, "bias_rows")
         ident = held([P, P], F32, "ident")
         bias = held([P, 8], F32, "bias")
 
-        nc.vector.memset(tab_sc[:].bitcast(I32), 0)
-        nc.gpsimd.memset(tab2_sc[:].bitcast(I32), 0)
         nc.vector.memset(bias_rows[:], 0.0)
         make_identity(nc, ident[:])
         nc.gpsimd.memset(w1s_raw[:], 0)
         for g in range(2):
-            nc.vector.memset(v_sc[g][:].bitcast(I32), 0)
+            nc.gpsimd.memset(v_sc[g][:].bitcast(I32), 0)
 
         def words(dram):
             return dram.rearrange("p t i -> p (t i)").bitcast(I32)
@@ -76,14 +77,14 @@ def tile_list_wax_crack_scores_kernel(
         def load_w2(b):
             nc.sync.dma_start(w2_raw[b][:], w2[:, 512 * b : 512 * (b + 1)].rearrange("(p j) c -> p j c", j=4))
 
-        def load_w3(b, tag):
-            w3_raw.append(held([P, 4, 512], F32, "w3_raw%d" % b, tag))
+        def load_w3(b, offset):
+            w3_raw.append(shared.tile([P, 4, 512], F32, name="w3_raw%d" % b, offset=offset, align_bytes=64))
             rows = w3[512 * b : 512 * (b + 1), :].rearrange("(m t s) n -> s m t n", t=4, s=4)
             for s in range(4):
                 nc.sync.dma_start(w3_raw[b][s:P:4, :, :], rows[s])
 
-        def load_page(n, tag):
-            page.append(held([P, T2], F32, "page%d" % n, tag))
+        def load_page(n, offset):
+            page.append(shared.tile([P, T2], F32, name="page%d" % n, offset=offset, align_bytes=64))
             nc.sync.dma_start(page[n][:], page1[P * n : P * (n + 1), :])
 
         def gather_words(dst, table, lst, u):
@@ -110,43 +111,53 @@ def tile_list_wax_crack_scores_kernel(
 
         sines = {}
 
-        def wax_side(q, b):
-            u, c0 = divmod(q * Q, HALF)
-            sine = held([P, 4, Q], F32, "sine%d_%d" % (q, b))
-            for pair in range(2):
-                wax = psum.tile([P, 2, Q], F32, name="wax", tag="wax")
-                for e in range(2):
-                    t = 2 * pair + e
-                    nc.tensor.matmul_mx(
-                        out=wax[:, e, :],
-                        lhsT=w2_c[b][:, P * t : P * (t + 1)].bitcast(FP8X4),
-                        lhsT_scale=w2_s[b][:, P * t : P * (t + 1)],
-                        rhs=v2_w[u][:, c0 : c0 + Q].bitcast(FP8X4),
-                        rhs_scale=v2_sc[:, q * Q : (q + 1) * Q],
-                        start=True, stop=True,
-                    )
-                for e in range(2):
-                    t = 2 * pair + e
-                    nc.scalar.activation(
-                        sine[:, t, :], wax[:, e, :], ACT.Sin, bias=bias[:, 4 * b + t : 4 * b + t + 1], scale=1.0
-                    )
-            sines[(q, b)] = sine
+        def wax_side(u, b):
+            sine = held([P, 4, HALF], F32, "sine%d_%d" % (u, b), "sine%d_%d" % (u, b))
+            for t in range(4):
+                wax = psum.tile([P, HALF], F32, name="wax", tag="wax")
+                nc.tensor.matmul_mx(
+                    out=wax[:],
+                    lhsT=w2_c[b][:, P * t : P * (t + 1)].bitcast(FP8X4),
+                    lhsT_scale=w2_s[b][:, P * t : P * (t + 1)],
+                    rhs=v2_w[u][:].bitcast(FP8X4),
+                    rhs_scale=v2_sc[:, u * HALF : (u + 1) * HALF],
+                    start=True, stop=True,
+                )
+                nc.scalar.activation(
+                    sine[:, t, :], wax[:], ACT.Sin, bias=bias[:, 4 * b + t : 4 * b + t + 1], scale=1.0
+                )
+            sines[(u, b)] = sine
+
+        def load_tab2_scale_row(r):
+            nc.sync.dma_start(
+                tab2_sc[r:P:4, :].bitcast(I32),
+                tab2_scales[0, r:16:4, :].bitcast(I32).unsqueeze(1).to_broadcast([4, 8, T // 4]),
+            )
+
+        def move_scale_rows(g, d):
+            nc.sync.dma_start(
+                v_sc[g][32 * d : 32 * d + 4, :].bitcast(I32),
+                got_sc[32 * d + g : 32 * (d + 1) : 8, :].bitcast(I32),
+            )
 
         nc.sync.dma_start(list1[:], offs)
-        nc.sync.dma_start(list2[:], offs2)
         for g in range(2):
-            nc.scalar.dma_start(tab_sc[g:P:8, :].bitcast(I32), tab_scales[g].bitcast(I32))
+            nc.sync.dma_start(
+                tab_sc[g:P:2, :].bitcast(I32), tab_scales[g].bitcast(I32).unsqueeze(1).to_broadcast([16, 4, T // 4])
+            )
         nc.sync.dma_start(tab2w[:], words(tab2_words[0]))
+        nc.sync.dma_start(list2[:], offs2)
+        load_tab2_scale_row(0)
+        load_tab2_scale_row(1)
         load_w2(0)
+        load_tab2_scale_row(2)
+        load_tab2_scale_row(3)
+        nc.sync.dma_start(tabw[0][:], words(tab_words[0]))
         nc.sync.dma_start(list3[:], offs3)
         for b in range(2):
-            nc.scalar.dma_start(
+            nc.gpsimd.dma_start(
                 bias_rows[4 * b : 4 * b + 4, :].rearrange("t (m s) -> t m s", s=4),
                 b2[512 * b : 512 * (b + 1)].rearrange("(m t s) -> t m s", t=4, s=4),
-            )
-        for d in range(4):
-            nc.scalar.dma_start(
-                tab2_sc[32 * d : 32 * d + 4, :].bitcast(I32), tab2_scales[0, 4 * d : 4 * d + 4, :].bitcast(I32)
             )
         for d in range(4):
             nc.gpsimd.dma_start(
@@ -155,37 +166,40 @@ def tile_list_wax_crack_scores_kernel(
             )
 
         nc.vector.tensor_copy(got_sc[:], tab_sc[:].indirect(list1[:]))
-        tabw.append(held([P, T], I32, "tabw0", "slot_c"))
-        nc.sync.dma_start(tabw[0][:], words(tab_words[0]))
         turned = psum.tile([P, 2, Q], F32, name="turned", tag="y")
         nc.tensor.transpose(turned[:, 0, 0:P], bias_rows[:], ident[:])
         nc.scalar.copy(bias[:], turned[:, 0, 0:8])
-        w1_raw = held([P, 2 * H // 2], I32, "w1_raw", "slot_f")
+        tabw.append(shared.tile([P, T], I32, name="tabw1", offset=8192, align_bytes=64))
+        w1_raw = shared.tile([P, 2 * H // 2], I32, name="w1_raw", offset=4096, align_bytes=64)
+        moves = [(g, d) for g in range(2) for d in range(4)]
+        for g, d in moves[0:2]:
+            move_scale_rows(g, d)
+        nc.sync.dma_start(tabw[1][:], words(tab_words[1]))
+        for g, d in moves[2:5]:
+            move_scale_rows(g, d)
         nc.sync.dma_start(
             w1_raw[:].rearrange("p (g c) -> p g c", g=2), w1_words.bitcast(I32).rearrange("g p c -> p g c")
         )
-        for g in range(2):
-            for d in range(4):
-                nc.sync.dma_start(
-                    v_sc[g][32 * d : 32 * d + 4, :].bitcast(I32),
-                    got_sc[32 * d + g : 32 * (d + 1) : 8, :].bitcast(I32),
-                )
+        for g, d in moves[5:8]:
+            move_scale_rows(g, d)
         gather_words(v2_w[0], tab2w, list2, 0)
         gather_words(v2_w[1], tab2w, list2, 1)
+        w2_raw.append(shared.tile([P, 4, 512], F32, name="w2_raw1", offset=16384, align_bytes=64))
+        load_w2(1)
+        load_w3(0, 24576)
         nc.vector.tensor_copy(v2_sc[:], tab2_sc[:].indirect(list2[:]))
-        tabw.append(held([P, T], I32, "tabw1", "slot_a"))
-        nc.sync.dma_start(tabw[1][:], words(tab_words[1]))
+        load_w3(1, 32768)
+        gain = shared.tile([P, S], F32, name="gain", offset=40960, align_bytes=64)
+        nc.sync.dma_start(gain[:], wgo)
         w2_bf = round_w2(0)
         quantise(w2_c[0][:], w2_s[0][:], w2_bf[:])
-        w2_raw.append(held([P, 4, 512], F32, "w2_raw1", "slot_b"))
-        load_w2(1)
-        load_w3(0, "slot_d")
         gather_words(v_w[0][0], tabw[0], list1, 0)
         gather_words(v_w[0][1], tabw[0], list1, 1)
-        load_w3(1, "slot_c")
+        load_page(0, 45056)
+        load_page(1, 53248)
+        for u in range(2):
+            wax_side(u, 0)
         w2_bf = round_w2(1)
-        for q in range(4):
-            wax_side(q, 0)
         gather_words(v_w[1][0], tabw[1], list1, 0)
         nc.vector.tensor_copy(
             w1_s[:].rearrange("p (g t m) -> p g t m", t=4, m=32),
@@ -195,67 +209,69 @@ def tile_list_wax_crack_scores_kernel(
             w1_c[:].rearrange("p (g t m e) -> p g t m e", t=4, m=32, e=2),
             w1_raw[:].rearrange("p (g m t e) -> p g t m e", t=4, m=32, e=2),
         )
-        quantise(w2_c[1][:], w2_s[1][:], w2_bf[:])
+        load_page(2, 0)
+        load_page(3, 61440)
         gather_words(v_w[1][1], tabw[1], list1, 1)
-        gain = held([P, S], F32, "gain", "slot_e")
-        nc.sync.dma_start(gain[:], wgo)
-        load_page(0, "slot_a")
-        load_page(1, "slot_b")
 
         w1_codes = w1_c[:].bitcast(U8)
         w1_scale = w1_s[:].bitcast(U8)
 
         def front(unit):
-            q, b = divmod(unit, 2)
+            q, b = UNITS[unit]
             u, c0 = divmod(q * Q, HALF)
-            if b == 1:
-                wax_side(q, b)
-            sine = sines[(q, b)]
+            sine = sines[(u, b)][:, :, c0 : c0 + Q]
             cloth_bf = ring.tile([P, 4 * Q], BF16, name="cloth_bf", align_bytes=64)
             banks = []
             for x in range(2):
-                cloth = psum.tile([P, 4, P], F32, name="cloth", tag="cloth", bufs=4)
-                j0 = q * Q + P * x
-                for t in range(4):
+                cloth = psum.tile([P, 2, Q], F32, name="cloth", tag="cloth", bufs=4)
+                for e in range(2):
                     for g in range(2):
-                        col = H * g + 512 * b + P * t
+                        col = H * g + 512 * b + P * (2 * x + e)
                         nc.tensor.matmul_mx(
-                            out=cloth[:, t, :],
+                            out=cloth[:, e, :],
                             lhsT=w1_codes[:, 2 * col : 2 * (col + P)].bitcast(FP4X4),
                             lhsT_scale=w1_scale[:, col : col + P],
-                            rhs=v_w[g][u][:, c0 + P * x : c0 + P * (x + 1)].bitcast(FP8X4),
-                            rhs_scale=v_sc[g][:, j0 : j0 + P],
+                            rhs=v_w[g][u][:, c0 : c0 + Q].bitcast(FP8X4),
+                            rhs_scale=v_sc[g][:, q * Q : (q + 1) * Q],
                             start=(g == 0), stop=(g == 1),
                         )
                 nc.scalar.copy(
-                    cloth_bf[:, 512 * x : 512 * (x + 1)].rearrange("p (j t) -> p j t", t=4),
-                    cloth[:].rearrange("p t j -> p j t"),
+                    cloth_bf[:, 512 * x : 512 * (x + 1)].rearrange("p (j e) -> p j e", e=2),
+                    cloth[:].rearrange("p e j -> p j e"),
                 )
                 banks.append(cloth)
-            prod = ring.tile([P, 4 * Q], BF16, name="prod", align_bytes=64)
-            return {"sine": sine, "cloth_bf": cloth_bf, "banks": banks, "prod": prod}
+            return {"sine": sine, "cloth_bf": cloth_bf, "banks": banks}
 
         def multiply(st, x):
             nc.vector.tensor_tensor(
-                st["prod"][:, 512 * x : 512 * (x + 1)].rearrange("p (c i t) -> p c t i", i=2, t=4),
-                st["banks"][x][:].rearrange("p t (c i) -> p c t i", i=2),
-                st["sine"][:, :, P * x : P * (x + 1)].rearrange("p t (c i) -> p c t i", i=2),
+                st["prod"][:, 512 * x : 512 * (x + 1)].rearrange("p (j e) -> p j e", e=2),
+                st["banks"][x][:].rearrange("p e j -> p j e"),
+                st["sine"][:, 2 * x : 2 * x + 2, :].rearrange("p e j -> p j e"),
                 ALU.mult,
             )
 
         def larger(st):
             h_bf = ring.tile([P, 4 * Q], BF16, name="h_bf", bufs=2, align_bytes=64)
-            nc.vector.tensor_tensor(h_bf[:], st["prod"][:], st["cloth_bf"][:], ALU.max)
+            nc.vector.tensor_tensor(
+                h_bf[:].rearrange("p (j x e) -> p j x e", x=2, e=2),
+                st["prod"][:].rearrange("p (x j e) -> p j x e", x=2, e=2),
+                st["cloth_bf"][:].rearrange("p (x j e) -> p j x e", x=2, e=2),
+                ALU.max,
+            )
             st["h_bf"] = h_bf
 
         def quantise_h(st):
-            h_c = ring.tile([P, Q], U32, name="h_c", bufs=4, align_bytes=64)
-            h_s = ring.tile([P, Q], U8, name="h_s", bufs=4, align_bytes=64)
+            h_c = ring.tile([P, Q], U32, name="h_c", bufs=8, align_bytes=64)
+            h_s = ring.tile([P, Q], U8, name="h_s", bufs=8, align_bytes=64)
             quantise(h_c[:], h_s[:], st["h_bf"][:])
             st["h_c"], st["h_s"] = h_c, h_s
 
         def second_product(q, pair_of_units):
-            u, c0 = divmod(q * Q, HALF)
+            if q < 2:
+                y_early.append(held([P, 4, Q], F32, "y_early%d" % q, "sine1_1" if q else ""))
+                y_sb = y_early[q][:]
+            else:
+                y_sb = y_late[:, :, (q - 2) * Q : (q - 1) * Q]
             for pair in range(2):
                 y = psum.tile([P, 2, Q], F32, name="y", tag="y")
                 for e in range(2):
@@ -269,13 +285,12 @@ def tile_list_wax_crack_scores_kernel(
                             rhs_scale=pair_of_units[b]["h_s"][:],
                             start=(b == 0), stop=(b == 1),
                         )
-                nc.scalar.copy(y_sb[u][:, 2 * pair : 2 * pair + 2, c0 : c0 + Q], y[:])
+                nc.scalar.copy(y_sb[:, 2 * pair : 2 * pair + 2, :], y[:])
 
         def scatter(n, j0, width):
-            u, c0 = divmod(j0, HALF)
             nc.vector.tensor_tensor(
                 page[n][:].indirect(list3[:, j0 // 16 : (j0 + width) // 16]),
-                y_sb[u][:, n, c0 : c0 + width],
+                y_late[:, n, :] if width == HALF else y_early[j0 // Q][:, n, :],
                 gain[:, j0 : j0 + width],
                 ALU.mult,
             )
@@ -283,36 +298,38 @@ def tile_list_wax_crack_scores_kernel(
         def store(n):
             nc.sync.dma_start(out[P * n : P * (n + 1), :], page[n][:])
 
-        early = {4: [(0, 0), (1, 0)], 5: [(2, 0), (3, 0)], 6: [(0, 1), (1, 1)], 7: [(2, 1)]}
         units = [front(0)]
         for unit in range(8):
             if unit + 1 < 8:
                 units.append(front(unit + 1))
-            if unit in (0, 1):
-                w3_bf = round_w3(unit)
-                load_page(2 + unit, ("slot_d", "slot_c")[unit])
-            for n, q in early.get(unit, []):
-                scatter(n, q * Q, Q)
+            if unit in (0, 2):
+                w3_bf = round_w3(unit // 2)
+            if unit in (1, 3):
+                wax_side(unit // 2, 1)
+            if unit >= 6:
+                scatter(2 * (unit - 6), 0, Q)
+                scatter(2 * (unit - 6) + 1, 0, Q)
+            units[unit]["prod"] = ring.tile([P, 4 * Q], BF16, name="prod", bufs=2, align_bytes=64)
             multiply(units[unit], 0)
             if unit > 0:
                 larger(units[unit - 1])
+            else:
+                quantise(w2_c[1][:], w2_s[1][:], w2_bf[:])
             multiply(units[unit], 1)
             if unit > 0:
                 quantise_h(units[unit - 1])
-            if unit in (0, 1):
-                quantise(w3_c[unit][:], w3_s[unit][:], w3_bf[:])
-            if unit > 0 and unit % 2 == 0:
-                second_product(unit // 2 - 1, units[unit - 2 : unit])
-        scatter(3, Q, Q)
+            if unit in (1, 3):
+                quantise(w3_c[unit // 2][:], w3_s[unit // 2][:], w3_bf[:])
+            if unit == 5:
+                second_product(0, [units[0], units[4]])
+        second_product(1, [units[1], units[5]])
+        second_product(2, [units[2], units[6]])
         larger(units[7])
-        scatter(0, 2 * Q, Q)
+        scatter(0, Q, Q)
         quantise_h(units[7])
-        second_product(3, units[6:8])
-        scatter(1, 2 * Q, Q)
-        scatter(0, 3 * Q, Q)
-        store(0)
-        scatter(1, 3 * Q, Q)
-        store(1)
-        for n in (2, 3):
-            scatter(n, 2 * Q, 2 * Q)
+        second_product(3, [units[3], units[7]])
+        for n in (1, 2, 3):
+            scatter(n, Q, Q)
+        for n in range(4):
+            scatter(n, HALF, HALF)
             store(n)

@@ -20,7 +20,7 @@ ACT = mybir.ActivationFunctionType
 P = 128
 Q = 256
 HALF = 512
-UNITS = [(q, b) for b in range(2) for q in range(4)]
+UNITS = [(u, b) for b in range(2) for u in range(2)]
 
 
 def tile_list_wax_crack_scores_kernel(
@@ -47,10 +47,10 @@ def tile_list_wax_crack_scores_kernel(
         got_sc = held([P, S], U8, "got_sc")
         v2_sc = held([P, S], U8, "v2_sc")
         v_sc = [held([P, S], U8, "v_sc%d" % g) for g in range(2)]
-        v_w = [[held([P, HALF], U32, "v_w%d_%d" % (g, u)) for u in range(2)] for g in range(2)]
-        v2_w = [held([P, HALF], U32, "v2_w%d" % u) for u in range(2)]
-        w1_c = held([P, 2 * H // 2], I32, "w1_c")
+        v_w = [held([P, S], U32, "v_w%d" % g) for g in range(2)]
+        v2_w = held([P, S], U32, "v2_w")
         w1s_raw = shared.tile([P, 2 * H // 4], I32, name="w1s_raw", offset=61440, align_bytes=64)
+        w1_c = held([P, 2 * H // 2], I32, "w1_c")
         w1_s = held([P, 2 * H // 4], I32, "w1_s")
         w2_raw = [held([P, 4, 512], F32, "w2_raw0")]
         w3_raw = []
@@ -59,17 +59,17 @@ def tile_list_wax_crack_scores_kernel(
         w2_s = [held([P, 512], U8, "w2_s%d" % b) for b in range(2)]
         w3_c = [held([P, 512], U32, "w3_c%d" % b) for b in range(2)]
         w3_s = [held([P, 512], U8, "w3_s%d" % b) for b in range(2)]
-        y_late = held([P, 4, HALF], F32, "y_late")
-        y_early = []
+        y_sb = held([P, 4, S], F32, "y_sb")
+        last_prod = held([P, 2 * HALF], F32, "last_prod")
         bias_rows = held([P, P], F32, "bias_rows")
         ident = held([P, P], F32, "ident")
         bias = held([P, 8], F32, "bias")
 
         nc.vector.memset(bias_rows[:], 0.0)
         make_identity(nc, ident[:])
-        nc.gpsimd.memset(w1s_raw[:], 0)
+        nc.vector.memset(w1s_raw[:], 0)
         for g in range(2):
-            nc.gpsimd.memset(v_sc[g][:].bitcast(I32), 0)
+            nc.vector.memset(v_sc[g][:].bitcast(I32), 0)
 
         def words(dram):
             return dram.rearrange("p t i -> p (t i)").bitcast(I32)
@@ -87,8 +87,8 @@ def tile_list_wax_crack_scores_kernel(
             page.append(shared.tile([P, T2], F32, name="page%d" % n, offset=offset, align_bytes=64))
             nc.sync.dma_start(page[n][:], page1[P * n : P * (n + 1), :])
 
-        def gather_words(dst, table, lst, u):
-            nc.vector.tensor_copy(dst[:], table[:].bitcast(U32).indirect(lst[:, 32 * u : 32 * (u + 1)]))
+        def gather_words(dst, table, lst, j0, j1):
+            nc.vector.tensor_copy(dst[:, j0:j1], table[:].bitcast(U32).indirect(lst[:, j0 // 16 : j1 // 16]))
 
         def round_w2(b):
             grouped = ring.tile([P, 2048], BF16, name="w2_bf", tag="grouped", bufs=2, align_bytes=64)
@@ -119,7 +119,7 @@ def tile_list_wax_crack_scores_kernel(
                     out=wax[:],
                     lhsT=w2_c[b][:, P * t : P * (t + 1)].bitcast(FP8X4),
                     lhsT_scale=w2_s[b][:, P * t : P * (t + 1)],
-                    rhs=v2_w[u][:].bitcast(FP8X4),
+                    rhs=v2_w[:, u * HALF : (u + 1) * HALF].bitcast(FP8X4),
                     rhs_scale=v2_sc[:, u * HALF : (u + 1) * HALF],
                     start=True, stop=True,
                 )
@@ -153,14 +153,14 @@ def tile_list_wax_crack_scores_kernel(
         load_tab2_scale_row(2)
         load_tab2_scale_row(3)
         nc.sync.dma_start(tabw[0][:], words(tab_words[0]))
-        nc.sync.dma_start(list3[:], offs3)
         for b in range(2):
-            nc.gpsimd.dma_start(
+            nc.scalar.dma_start(
                 bias_rows[4 * b : 4 * b + 4, :].rearrange("t (m s) -> t m s", s=4),
                 b2[512 * b : 512 * (b + 1)].rearrange("(m t s) -> t m s", t=4, s=4),
             )
+        nc.sync.dma_start(list3[:], offs3)
         for d in range(4):
-            nc.gpsimd.dma_start(
+            nc.sync.dma_start(
                 w1s_raw[32 * d : 32 * d + 4, :].rearrange("p (g c) -> p g c", g=2),
                 w1_scales[:, 4 * d : 4 * d + 4, :].bitcast(I32).rearrange("g r c -> r g c"),
             )
@@ -169,8 +169,8 @@ def tile_list_wax_crack_scores_kernel(
         turned = psum.tile([P, 2, Q], F32, name="turned", tag="y")
         nc.tensor.transpose(turned[:, 0, 0:P], bias_rows[:], ident[:])
         nc.scalar.copy(bias[:], turned[:, 0, 0:8])
-        tabw.append(shared.tile([P, T], I32, name="tabw1", offset=8192, align_bytes=64))
         w1_raw = shared.tile([P, 2 * H // 2], I32, name="w1_raw", offset=4096, align_bytes=64)
+        tabw.append(shared.tile([P, T], I32, name="tabw1", offset=8192, align_bytes=64))
         moves = [(g, d) for g in range(2) for d in range(4)]
         for g, d in moves[0:2]:
             move_scale_rows(g, d)
@@ -182,8 +182,7 @@ def tile_list_wax_crack_scores_kernel(
         )
         for g, d in moves[5:8]:
             move_scale_rows(g, d)
-        gather_words(v2_w[0], tab2w, list2, 0)
-        gather_words(v2_w[1], tab2w, list2, 1)
+        gather_words(v2_w, tab2w, list2, 0, S)
         w2_raw.append(shared.tile([P, 4, 512], F32, name="w2_raw1", offset=16384, align_bytes=64))
         load_w2(1)
         load_w3(0, 24576)
@@ -193,14 +192,13 @@ def tile_list_wax_crack_scores_kernel(
         nc.sync.dma_start(gain[:], wgo)
         w2_bf = round_w2(0)
         quantise(w2_c[0][:], w2_s[0][:], w2_bf[:])
-        gather_words(v_w[0][0], tabw[0], list1, 0)
-        gather_words(v_w[0][1], tabw[0], list1, 1)
+        gather_words(v_w[0], tabw[0], list1, 0, S)
         load_page(0, 45056)
         load_page(1, 53248)
         for u in range(2):
             wax_side(u, 0)
         w2_bf = round_w2(1)
-        gather_words(v_w[1][0], tabw[1], list1, 0)
+        gather_words(v_w[1], tabw[1], list1, 0, HALF)
         nc.vector.tensor_copy(
             w1_s[:].rearrange("p (g t m) -> p g t m", t=4, m=32),
             w1s_raw[:].rearrange("p (g m t) -> p g t m", t=4, m=32),
@@ -209,127 +207,129 @@ def tile_list_wax_crack_scores_kernel(
             w1_c[:].rearrange("p (g t m e) -> p g t m e", t=4, m=32, e=2),
             w1_raw[:].rearrange("p (g m t e) -> p g t m e", t=4, m=32, e=2),
         )
-        load_page(2, 0)
-        load_page(3, 61440)
-        gather_words(v_w[1][1], tabw[1], list1, 1)
+        load_page(2, 61440)
+        load_page(3, 0)
+        gather_words(v_w[1], tabw[1], list1, HALF, S)
 
         w1_codes = w1_c[:].bitcast(U8)
         w1_scale = w1_s[:].bitcast(U8)
 
-        def front(unit):
-            q, b = UNITS[unit]
-            u, c0 = divmod(q * Q, HALF)
-            sine = sines[(u, b)][:, :, c0 : c0 + Q]
-            cloth_bf = ring.tile([P, 4 * Q], BF16, name="cloth_bf", align_bytes=64)
-            banks = []
-            for x in range(2):
-                cloth = psum.tile([P, 2, Q], F32, name="cloth", tag="cloth", bufs=4)
-                for e in range(2):
-                    for g in range(2):
-                        col = H * g + 512 * b + P * (2 * x + e)
-                        nc.tensor.matmul_mx(
-                            out=cloth[:, e, :],
-                            lhsT=w1_codes[:, 2 * col : 2 * (col + P)].bitcast(FP4X4),
-                            lhsT_scale=w1_scale[:, col : col + P],
-                            rhs=v_w[g][u][:, c0 : c0 + Q].bitcast(FP8X4),
-                            rhs_scale=v_sc[g][:, q * Q : (q + 1) * Q],
-                            start=(g == 0), stop=(g == 1),
-                        )
-                nc.scalar.copy(
-                    cloth_bf[:, 512 * x : 512 * (x + 1)].rearrange("p (j e) -> p j e", e=2),
-                    cloth[:].rearrange("p e j -> p j e"),
-                )
-                banks.append(cloth)
-            return {"sine": sine, "cloth_bf": cloth_bf, "banks": banks}
+        def cloth_side(st, step):
+            u, b = st["unit"]
+            part, x = divmod(step, 2)
+            j0 = u * HALF + part * Q
+            cloth = psum.tile([P, 2, Q], F32, name="cloth", tag="cloth", bufs=4)
+            for e in range(2):
+                for g in range(2):
+                    col = H * g + 512 * b + P * (2 * x + e)
+                    nc.tensor.matmul_mx(
+                        out=cloth[:, e, :],
+                        lhsT=w1_codes[:, 2 * col : 2 * (col + P)].bitcast(FP4X4),
+                        lhsT_scale=w1_scale[:, col : col + P],
+                        rhs=v_w[g][:, j0 : j0 + Q].bitcast(FP8X4),
+                        rhs_scale=v_sc[g][:, j0 : j0 + Q],
+                        start=(g == 0), stop=(g == 1),
+                    )
+            nc.scalar.copy(piece(st["cloth_bf"], step), cloth[:].rearrange("p e j -> p j e"))
+            st["banks"].append(cloth)
 
-        def multiply(st, x):
+        def piece(pairs, step):
+            part, x = divmod(step, 2)
+            return pairs.rearrange("p (x j e) -> p x j e", x=2, e=2)[:, x, part * Q : (part + 1) * Q, :]
+
+        def multiply(st, step):
+            part, x = divmod(step, 2)
             nc.vector.tensor_tensor(
-                st["prod"][:, 512 * x : 512 * (x + 1)].rearrange("p (j e) -> p j e", e=2),
-                st["banks"][x][:].rearrange("p e j -> p j e"),
-                st["sine"][:, 2 * x : 2 * x + 2, :].rearrange("p e j -> p j e"),
+                piece(st["prod"], step),
+                st["banks"][step][:].rearrange("p e j -> p j e"),
+                sines[st["unit"]][:, 2 * x : 2 * x + 2, part * Q : (part + 1) * Q].rearrange("p e j -> p j e"),
                 ALU.mult,
             )
 
         def larger(st):
-            h_bf = ring.tile([P, 4 * Q], BF16, name="h_bf", bufs=2, align_bytes=64)
+            h_bf = ring.tile([P, 4 * HALF], BF16, name="h_bf", bufs=2, align_bytes=64)
             nc.vector.tensor_tensor(
                 h_bf[:].rearrange("p (j x e) -> p j x e", x=2, e=2),
-                st["prod"][:].rearrange("p (x j e) -> p j x e", x=2, e=2),
-                st["cloth_bf"][:].rearrange("p (x j e) -> p j x e", x=2, e=2),
+                st["prod"].rearrange("p (x j e) -> p j x e", x=2, e=2),
+                st["cloth_bf"].rearrange("p (x j e) -> p j x e", x=2, e=2),
                 ALU.max,
             )
             st["h_bf"] = h_bf
 
         def quantise_h(st):
-            h_c = ring.tile([P, Q], U32, name="h_c", bufs=8, align_bytes=64)
-            h_s = ring.tile([P, Q], U8, name="h_s", bufs=8, align_bytes=64)
+            h_c = ring.tile([P, HALF], U32, name="h_c", bufs=4, align_bytes=64)
+            h_s = ring.tile([P, HALF], U8, name="h_s", bufs=4, align_bytes=64)
             quantise(h_c[:], h_s[:], st["h_bf"][:])
             st["h_c"], st["h_s"] = h_c, h_s
 
-        def second_product(q, pair_of_units):
-            if q < 2:
-                y_early.append(held([P, 4, Q], F32, "y_early%d" % q, "sine1_1" if q else ""))
-                y_sb = y_early[q][:]
-            else:
-                y_sb = y_late[:, :, (q - 2) * Q : (q - 1) * Q]
-            for pair in range(2):
-                y = psum.tile([P, 2, Q], F32, name="y", tag="y")
-                for e in range(2):
-                    n = 2 * pair + e
-                    for b in range(2):
-                        nc.tensor.matmul_mx(
-                            out=y[:, e, :],
-                            lhsT=w3_c[b][:, P * n : P * (n + 1)].bitcast(FP8X4),
-                            lhsT_scale=w3_s[b][:, P * n : P * (n + 1)],
-                            rhs=pair_of_units[b]["h_c"][:].bitcast(FP8X4),
-                            rhs_scale=pair_of_units[b]["h_s"][:],
-                            start=(b == 0), stop=(b == 1),
-                        )
-                nc.scalar.copy(y_sb[:, 2 * pair : 2 * pair + 2, :], y[:])
+        def y_rows(n, j0, j1):
+            if n == 1 and j0 == 0:
+                return last_prod[:, 0:HALF]
+            return y_sb[:, n, j0:j1]
 
-        def scatter(n, j0, width):
+        def second_product(u, n):
+            y = psum.tile([P, HALF], F32, name="y", tag="y")
+            for b in range(2):
+                nc.tensor.matmul_mx(
+                    out=y[:],
+                    lhsT=w3_c[b][:, P * n : P * (n + 1)].bitcast(FP8X4),
+                    lhsT_scale=w3_s[b][:, P * n : P * (n + 1)],
+                    rhs=units[2 * b + u]["h_c"][:].bitcast(FP8X4),
+                    rhs_scale=units[2 * b + u]["h_s"][:],
+                    start=(b == 0), stop=(b == 1),
+                )
+            nc.scalar.copy(y_rows(n, u * HALF, (u + 1) * HALF), y[:])
+
+        def scatter(n, j0, j1):
             nc.vector.tensor_tensor(
-                page[n][:].indirect(list3[:, j0 // 16 : (j0 + width) // 16]),
-                y_late[:, n, :] if width == HALF else y_early[j0 // Q][:, n, :],
-                gain[:, j0 : j0 + width],
-                ALU.mult,
+                page[n][:].indirect(list3[:, j0 // 16 : j1 // 16]), y_rows(n, j0, j1), gain[:, j0:j1], ALU.mult
             )
 
         def store(n):
             nc.sync.dma_start(out[P * n : P * (n + 1), :], page[n][:])
 
-        units = [front(0)]
-        for unit in range(8):
-            if unit + 1 < 8:
-                units.append(front(unit + 1))
-            if unit in (0, 2):
-                w3_bf = round_w3(unit // 2)
-            if unit in (1, 3):
-                wax_side(unit // 2, 1)
-            if unit >= 6:
-                scatter(2 * (unit - 6), 0, Q)
-                scatter(2 * (unit - 6) + 1, 0, Q)
-            units[unit]["prod"] = ring.tile([P, 4 * Q], BF16, name="prod", bufs=2, align_bytes=64)
-            multiply(units[unit], 0)
-            if unit > 0:
-                larger(units[unit - 1])
+        def open_unit(index):
+            cloth_bf = ring.tile([P, 4 * HALF], BF16, name="cloth_bf", align_bytes=64)
+            if index == 3:
+                prod = last_prod[:].bitcast(BF16)
             else:
+                prod = ring.tile([P, 4 * HALF], BF16, name="prod", bufs=2, align_bytes=64)[:]
+            units.append({"unit": UNITS[index], "cloth_bf": cloth_bf[:], "prod": prod, "banks": []})
+
+        units = []
+        open_unit(0)
+        cloth_side(units[0], 0)
+        cloth_side(units[0], 1)
+        for count in range(16):
+            index, step = divmod(count, 4)
+            ahead, ahead_step = divmod(count + 2, 4)
+            if ahead < 4:
+                if ahead_step == 0:
+                    open_unit(ahead)
+                cloth_side(units[ahead], ahead_step)
+            if count in (0, 4):
+                w3_bf = round_w3(count // 4)
+            if count in (2, 6):
+                wax_side(count // 4, 1)
+            multiply(units[index], step)
+            if count == 0:
                 quantise(w2_c[1][:], w2_s[1][:], w2_bf[:])
-            multiply(units[unit], 1)
-            if unit > 0:
-                quantise_h(units[unit - 1])
-            if unit in (1, 3):
-                quantise(w3_c[unit // 2][:], w3_s[unit // 2][:], w3_bf[:])
-            if unit == 5:
-                second_product(0, [units[0], units[4]])
-        second_product(1, [units[1], units[5]])
-        second_product(2, [units[2], units[6]])
-        larger(units[7])
-        scatter(0, Q, Q)
-        quantise_h(units[7])
-        second_product(3, [units[3], units[7]])
-        for n in (1, 2, 3):
-            scatter(n, Q, Q)
+            if count in (3, 7):
+                quantise(w3_c[count // 4][:], w3_s[count // 4][:], w3_bf[:])
+            if index > 0 and step == 0:
+                larger(units[index - 1])
+            if index > 0 and step == 1:
+                quantise_h(units[index - 1])
+            if count == 13:
+                for n in (0, 2, 3):
+                    second_product(0, n)
+        scatter(0, 0, HALF)
+        larger(units[3])
+        second_product(0, 1)
+        quantise_h(units[3])
         for n in range(4):
-            scatter(n, HALF, HALF)
+            second_product(1, n)
+        scatter(1, 0, HALF)
+        for n in range(4):
+            scatter(n, HALF if n < 2 else 0, S)
             store(n)

from contextlib import ExitStack

import concourse.mybir as mybir
from concourse.masks import make_identity

K, K2, H, N, T, S, T2 = 1024, 512, 1024, 512, 2048, 1024, 2048
FLOPS = 2 * S * (K * H + K2 * H + H * N)

F32 = mybir.dt.float32
BF16 = mybir.dt.bfloat16
I32 = mybir.dt.int32
U32 = mybir.dt.uint32
U16 = mybir.dt.uint16
U8 = mybir.dt.uint8
FP8X4 = mybir.dt.float8_e4m3fn_x4
FP4X4 = mybir.dt.float4_e2m1fn_x4
ALU = mybir.AluOpType
ACT = mybir.ActivationFunctionType

P = 128
Q = 256
HALF = 512
UNITS = [(u, b) for b in range(2) for u in range(2)]


def tile_list_wax_crack_scores_kernel(
    tc, tab_words, tab_scales, tab2_words, tab2_scales, w1_words, w1_scales,
    w2, b2, w3, page1, wgo, offs, offs2, offs3, out,
):
    nc = tc.nc
    with ExitStack() as ctx:
        keep = ctx.enter_context(tc.tile_pool(name="keep", bufs=1))
        shared = ctx.enter_context(tc.tile_pool(name="shared", bufs=1))
        ring = ctx.enter_context(tc.tile_pool(name="ring", bufs=3))
        psum = ctx.enter_context(tc.psum_pool(name="psum", bufs=2))

        def held(shape, dtype, name, tag=""):
            return keep.tile(shape, dtype, name=name, tag=tag, align_bytes=64)

        list1 = keep.tile([P, S // 16], U16, name="list1")
        list2 = keep.tile([P, S // 16], U16, name="list2")
        list3 = keep.tile([P, S // 16], U16, name="list3")
        tab_sc = shared.tile([P, T], U8, name="tab_sc", offset=7168, align_bytes=64)
        tab2_sc = shared.tile([P, T], U8, name="tab2_sc", offset=39936, align_bytes=64)
        tab2w = shared.tile([P, T], I32, name="tab2w", offset=20480, align_bytes=64)
        tabw = [shared.tile([P, T], I32, name="tabw0", offset=49152, align_bytes=64)]
        got_sc = held([P, S], U8, "got_sc")
        v2_sc = held([P, S], U8, "v2_sc")
        v_sc = [held([P, S], U8, "v_sc%d" % g) for g in range(2)]
        v_w = [held([P, S], U32, "v_w%d" % g) for g in range(2)]
        v2_w = held([P, S], U32, "v2_w")
        w1s_raw = shared.tile([P, 2 * H // 4], I32, name="w1s_raw", offset=61440, align_bytes=64)
        w1_c = held([P, 2 * H // 2], I32, "w1_c")
        w1_s = held([P, 2 * H // 4], I32, "w1_s")
        w2_raw = [held([P, 4, 512], F32, "w2_raw0")]
        w3_raw = []
        page = []
        w2_c = [held([P, 512], U32, "w2_c%d" % b) for b in range(2)]
        w2_s = [held([P, 512], U8, "w2_s%d" % b) for b in range(2)]
        w3_c = [held([P, 512], U32, "w3_c%d" % b) for b in range(2)]
        w3_s = [held([P, 512], U8, "w3_s%d" % b) for b in range(2)]
        y_sb = held([P, 4, S], F32, "y_sb")
        last_prod = held([P, 2 * HALF], F32, "last_prod")
        bias_rows = held([P, P], F32, "bias_rows")
        ident = held([P, P], F32, "ident")
        bias = held([P, 8], F32, "bias")

        nc.vector.memset(bias_rows[:], 0.0)
        make_identity(nc, ident[:])
        nc.vector.memset(w1s_raw[:], 0)
        for g in range(2):
            nc.vector.memset(v_sc[g][:].bitcast(I32), 0)

        def words(dram):
            return dram.rearrange("p t i -> p (t i)").bitcast(I32)

        def load_w2(b):
            nc.sync.dma_start(w2_raw[b][:], w2[:, 512 * b : 512 * (b + 1)].rearrange("(p j) c -> p j c", j=4))

        def load_w3(b, offset):
            w3_raw.append(shared.tile([P, 4, 512], F32, name="w3_raw%d" % b, offset=offset, align_bytes=64))
            rows = w3[512 * b : 512 * (b + 1), :].rearrange("(m t s) n -> s m t n", t=4, s=4)
            for s in range(4):
                nc.sync.dma_start(w3_raw[b][s:P:4, :, :], rows[s])

        def load_page(n, offset):
            page.append(shared.tile([P, T2], F32, name="page%d" % n, offset=offset, align_bytes=64))
            nc.sync.dma_start(page[n][:], page1[P * n : P * (n + 1), :])

        def gather_words(dst, table, lst, j0, j1):
            nc.vector.tensor_copy(dst[:, j0:j1], table[:].bitcast(U32).indirect(lst[:, j0 // 16 : j1 // 16]))

        def round_w2(b):
            grouped = ring.tile([P, 2048], BF16, name="w2_bf", tag="grouped", bufs=2, align_bytes=64)
            nc.scalar.copy(
                grouped[:].rearrange("p (t m i j) -> p t m j i", t=4, i=4, j=4),
                w2_raw[b][:].rearrange("p j (m t i) -> p t m j i", t=4, i=4),
            )
            return grouped

        def round_w3(b):
            grouped = ring.tile([P, 2048], BF16, name="w3_bf", tag="grouped", bufs=2, align_bytes=64)
            nc.scalar.copy(
                grouped[:].rearrange("p (c i t) -> p c t i", t=4, i=4),
                w3_raw[b][:].rearrange("p t (c i) -> p c t i", i=4),
            )
            return grouped

        def quantise(codes, scales, grouped):
            nc.vector.quantize_mx(out=codes.bitcast(FP8X4), scales=scales, in_=grouped)

        sines = {}

        def wax_side(u, b):
            sine = held([P, 4, HALF], F32, "sine%d_%d" % (u, b), "sine%d_%d" % (u, b))
            for t in range(4):
                wax = psum.tile([P, HALF], F32, name="wax", tag="wax")
                nc.tensor.matmul_mx(
                    out=wax[:],
                    lhsT=w2_c[b][:, P * t : P * (t + 1)].bitcast(FP8X4),
                    lhsT_scale=w2_s[b][:, P * t : P * (t + 1)],
                    rhs=v2_w[:, u * HALF : (u + 1) * HALF].bitcast(FP8X4),
                    rhs_scale=v2_sc[:, u * HALF : (u + 1) * HALF],
                    start=True, stop=True,
                )
                nc.scalar.activation(
                    sine[:, t, :], wax[:], ACT.Sin, bias=bias[:, 4 * b + t : 4 * b + t + 1], scale=1.0
                )
            sines[(u, b)] = sine

        def load_tab2_scale_row(r):
            nc.sync.dma_start(
                tab2_sc[r:P:4, :].bitcast(I32),
                tab2_scales[0, r:16:4, :].bitcast(I32).unsqueeze(1).to_broadcast([4, 8, T // 4]),
            )

        def move_scale_rows(g, d):
            nc.sync.dma_start(
                v_sc[g][32 * d : 32 * d + 4, :].bitcast(I32),
                got_sc[32 * d + g : 32 * (d + 1) : 8, :].bitcast(I32),
            )

        nc.sync.dma_start(list1[:], offs)
        for g in range(2):
            nc.sync.dma_start(
                tab_sc[g:P:2, :].bitcast(I32), tab_scales[g].bitcast(I32).unsqueeze(1).to_broadcast([16, 4, T // 4])
            )
        nc.sync.dma_start(tab2w[:], words(tab2_words[0]))
        nc.sync.dma_start(list2[:], offs2)
        load_tab2_scale_row(0)
        load_tab2_scale_row(1)
        load_w2(0)
        load_tab2_scale_row(2)
        load_tab2_scale_row(3)
        nc.sync.dma_start(tabw[0][:], words(tab_words[0]))
        for b in range(2):
            nc.scalar.dma_start(
                bias_rows[4 * b : 4 * b + 4, :].rearrange("t (m s) -> t m s", s=4),
                b2[512 * b : 512 * (b + 1)].rearrange("(m t s) -> t m s", t=4, s=4),
            )
        nc.sync.dma_start(list3[:], offs3)
        for d in range(4):
            nc.sync.dma_start(
                w1s_raw[32 * d : 32 * d + 4, :].rearrange("p (g c) -> p g c", g=2),
                w1_scales[:, 4 * d : 4 * d + 4, :].bitcast(I32).rearrange("g r c -> r g c"),
            )

        nc.vector.tensor_copy(got_sc[:], tab_sc[:].indirect(list1[:]))
        turned = psum.tile([P, 2, Q], F32, name="turned", tag="y")
        nc.tensor.transpose(turned[:, 0, 0:P], bias_rows[:], ident[:])
        nc.scalar.copy(bias[:], turned[:, 0, 0:8])
        w1_raw = shared.tile([P, 2 * H // 2], I32, name="w1_raw", offset=4096, align_bytes=64)
        tabw.append(shared.tile([P, T], I32, name="tabw1", offset=8192, align_bytes=64))
        moves = [(g, d) for g in range(2) for d in range(4)]
        for g, d in moves[0:2]:
            move_scale_rows(g, d)
        nc.sync.dma_start(tabw[1][:], words(tab_words[1]))
        for g, d in moves[2:5]:
            move_scale_rows(g, d)
        nc.sync.dma_start(
            w1_raw[:].rearrange("p (g c) -> p g c", g=2), w1_words.bitcast(I32).rearrange("g p c -> p g c")
        )
        for g, d in moves[5:8]:
            move_scale_rows(g, d)
        gather_words(v2_w, tab2w, list2, 0, S)
        w2_raw.append(shared.tile([P, 4, 512], F32, name="w2_raw1", offset=16384, align_bytes=64))
        load_w2(1)
        load_w3(0, 24576)
        nc.vector.tensor_copy(v2_sc[:], tab2_sc[:].indirect(list2[:]))
        load_w3(1, 32768)
        gain = shared.tile([P, S], F32, name="gain", offset=40960, align_bytes=64)
        nc.sync.dma_start(gain[:], wgo)
        w2_bf = round_w2(0)
        quantise(w2_c[0][:], w2_s[0][:], w2_bf[:])
        gather_words(v_w[0], tabw[0], list1, 0, S)
        load_page(0, 45056)
        load_page(1, 53248)
        for u in range(2):
            wax_side(u, 0)
        w2_bf = round_w2(1)
        gather_words(v_w[1], tabw[1], list1, 0, HALF)
        nc.vector.tensor_copy(
            w1_s[:].rearrange("p (g t m) -> p g t m", t=4, m=32),
            w1s_raw[:].rearrange("p (g m t) -> p g t m", t=4, m=32),
        )
        nc.vector.tensor_copy(
            w1_c[:].rearrange("p (g t m e) -> p g t m e", t=4, m=32, e=2),
            w1_raw[:].rearrange("p (g m t e) -> p g t m e", t=4, m=32, e=2),
        )
        load_page(2, 61440)
        load_page(3, 0)
        gather_words(v_w[1], tabw[1], list1, HALF, S)

        w1_codes = w1_c[:].bitcast(U8)
        w1_scale = w1_s[:].bitcast(U8)

        def cloth_side(st, step):
            u, b = st["unit"]
            part, x = divmod(step, 2)
            j0 = u * HALF + part * Q
            cloth = psum.tile([P, 2, Q], F32, name="cloth", tag="cloth", bufs=4)
            for e in range(2):
                for g in range(2):
                    col = H * g + 512 * b + P * (2 * x + e)
                    nc.tensor.matmul_mx(
                        out=cloth[:, e, :],
                        lhsT=w1_codes[:, 2 * col : 2 * (col + P)].bitcast(FP4X4),
                        lhsT_scale=w1_scale[:, col : col + P],
                        rhs=v_w[g][:, j0 : j0 + Q].bitcast(FP8X4),
                        rhs_scale=v_sc[g][:, j0 : j0 + Q],
                        start=(g == 0), stop=(g == 1),
                    )
            nc.scalar.copy(piece(st["cloth_bf"], step), cloth[:].rearrange("p e j -> p j e"))
            st["banks"].append(cloth)

        def piece(pairs, step):
            part, x = divmod(step, 2)
            return pairs.rearrange("p (x j e) -> p x j e", x=2, e=2)[:, x, part * Q : (part + 1) * Q, :]

        def multiply(st, step):
            part, x = divmod(step, 2)
            nc.vector.tensor_tensor(
                piece(st["prod"], step),
                st["banks"][step][:].rearrange("p e j -> p j e"),
                sines[st["unit"]][:, 2 * x : 2 * x + 2, part * Q : (part + 1) * Q].rearrange("p e j -> p j e"),
                ALU.mult,
            )

        def larger(st):
            h_bf = ring.tile([P, 4 * HALF], BF16, name="h_bf", bufs=2, align_bytes=64)
            nc.vector.tensor_tensor(
                h_bf[:].rearrange("p (j x e) -> p j x e", x=2, e=2),
                st["prod"].rearrange("p (x j e) -> p j x e", x=2, e=2),
                st["cloth_bf"].rearrange("p (x j e) -> p j x e", x=2, e=2),
                ALU.max,
            )
            st["h_bf"] = h_bf

        def quantise_h(st):
            h_c = ring.tile([P, HALF], U32, name="h_c", bufs=4, align_bytes=64)
            h_s = ring.tile([P, HALF], U8, name="h_s", bufs=4, align_bytes=64)
            quantise(h_c[:], h_s[:], st["h_bf"][:])
            st["h_c"], st["h_s"] = h_c, h_s

        def y_rows(n, j0, j1):
            if n == 1 and j0 == 0:
                return last_prod[:, 0:HALF]
            return y_sb[:, n, j0:j1]

        def second_product(u, n):
            y = psum.tile([P, HALF], F32, name="y", tag="y")
            for b in range(2):
                nc.tensor.matmul_mx(
                    out=y[:],
                    lhsT=w3_c[b][:, P * n : P * (n + 1)].bitcast(FP8X4),
                    lhsT_scale=w3_s[b][:, P * n : P * (n + 1)],
                    rhs=units[2 * b + u]["h_c"][:].bitcast(FP8X4),
                    rhs_scale=units[2 * b + u]["h_s"][:],
                    start=(b == 0), stop=(b == 1),
                )
            nc.scalar.copy(y_rows(n, u * HALF, (u + 1) * HALF), y[:])

        def scatter(n, j0, j1):
            nc.vector.tensor_tensor(
                page[n][:].indirect(list3[:, j0 // 16 : j1 // 16]), y_rows(n, j0, j1), gain[:, j0:j1], ALU.mult
            )

        def store(n):
            nc.sync.dma_start(out[P * n : P * (n + 1), :], page[n][:])

        def open_unit(index):
            cloth_bf = ring.tile([P, 4 * HALF], BF16, name="cloth_bf", align_bytes=64)
            if index == 3:
                prod = last_prod[:].bitcast(BF16)
            else:
                prod = ring.tile([P, 4 * HALF], BF16, name="prod", bufs=2, align_bytes=64)[:]
            units.append({"unit": UNITS[index], "cloth_bf": cloth_bf[:], "prod": prod, "banks": []})

        units = []
        open_unit(0)
        cloth_side(units[0], 0)
        cloth_side(units[0], 1)
        for count in range(16):
            index, step = divmod(count, 4)
            ahead, ahead_step = divmod(count + 2, 4)
            if ahead < 4:
                if ahead_step == 0:
                    open_unit(ahead)
                cloth_side(units[ahead], ahead_step)
            if count in (0, 4):
                w3_bf = round_w3(count // 4)
            if count in (2, 6):
                wax_side(count // 4, 1)
            multiply(units[index], step)
            if count == 0:
                quantise(w2_c[1][:], w2_s[1][:], w2_bf[:])
            if count in (3, 7):
                quantise(w3_c[count // 4][:], w3_s[count // 4][:], w3_bf[:])
            if index > 0 and step == 0:
                larger(units[index - 1])
            if index > 0 and step == 1:
                quantise_h(units[index - 1])
            if count == 13:
                for n in (0, 2, 3):
                    second_product(0, n)
        scatter(0, 0, HALF)
        larger(units[3])
        second_product(0, 1)
        quantise_h(units[3])
        for n in range(4):
            second_product(1, n)
        scatter(1, 0, HALF)
        for n in range(4):
            scatter(n, HALF if n < 2 else 0, S)
            store(n)
